import numpy as np
import ml_dtypes


def mxq(x, axis, fmt="e4m3"):
    dtype, down = {"e4m3": (ml_dtypes.float8_e4m3fn, 7), "e5m2": (ml_dtypes.float8_e5m2, 14)}[fmt]
    v = np.moveaxis(np.asarray(x, np.float32).astype(ml_dtypes.bfloat16).astype(np.float64), axis, -1)
    blocks = v.reshape(v.shape[:-1] + (-1, 32))
    amax = np.abs(blocks).max(-1, keepdims=True)
    byte = np.maximum(np.where(amax > 0, np.frexp(amax)[1] - 1 + 127, 0) - down, 1)
    scale = np.exp2(byte - 127.0)
    codes = (blocks / scale).astype(np.float32).astype(dtype).astype(np.float64)
    return np.moveaxis((codes * scale).reshape(v.shape), -1, axis)


WIDE = False


def mx_kscale(k):
    if not WIDE:
        return np.ones(k)
    levels = np.array([30, -30])
    if k % 512:
        return np.exp2(np.random.permutation(np.resize(levels, k // 32))).repeat(32)
    a = np.empty((k // 512, 16))
    for p in range(k // 512):
        a[p, :8] = np.random.permutation(np.resize(levels, 8))
        for g in range(8):
            far = levels[np.abs(levels - a[p, g]) >= 10]
            a[p, g + 8] = far[np.random.randint(len(far))]
    return np.exp2(a.ravel()).repeat(32)


def f64(x):
    return np.asarray(x).astype(np.float64)


def striped(idx):
    return np.tile(np.asarray(idx).reshape(-1, 16).T, (8, 1)).astype(np.uint16)


def unstriped(offs):
    return offs[:16].T.reshape(-1).astype(np.int64)


E2M1 = np.array([0.0, 0.5, 1.0, 1.5, 2.0, 3.0, 4.0, 6.0, -0.0, -0.5, -1.0, -1.5, -2.0, -3.0, -4.0, -6.0])


def pack_weight(w, fmt):
    k, n = w.shape
    w = f64(np.asarray(w, np.float32).astype(ml_dtypes.bfloat16)).reshape(k // 32, 32, n)
    amax = np.abs(w).max(1)
    if fmt in ("e4m3", "e5m2"):
        byte = np.frexp(amax)[1] - 1 + 127 - (7 if fmt == "e4m3" else 14)
    else:
        mant, ex = np.frexp(amax / 6.0)
        byte = np.where(mant > 0.5, ex, ex - 1) + 127
    byte = np.clip(np.where(amax > 0, byte, 1), 1, 254)
    scaled = (w * np.exp2(127.0 - byte)[:, None, :]).reshape(k, n).astype(np.float32)
    by_word = np.ascontiguousarray(scaled.reshape(k // 512, 128, 4, n).transpose(0, 1, 3, 2))
    if fmt in ("e4m3", "e5m2"):
        words = by_word.astype(ml_dtypes.float8_e4m3fn if fmt == "e4m3" else ml_dtypes.float8_e5m2).view(np.uint8)
    else:
        c = by_word.astype(ml_dtypes.float4_e2m1fn).view(np.uint8) & 0xF
        words = (c[..., 0::2] | (c[..., 1::2] << 4)).reshape(k // 512, 128, 2 * n)
    return np.ascontiguousarray(words), np.ascontiguousarray(byte.astype(np.uint8).reshape(k // 512, 16, n))


def unpack_weight(words, scales, fmt):
    g, _, n = scales.shape
    words = np.ascontiguousarray(words).reshape(g, 128, n, -1)
    if fmt in ("e4m3", "e5m2"):
        vals = words.view(ml_dtypes.float8_e4m3fn if fmt == "e4m3" else ml_dtypes.float8_e5m2).astype(np.float64)
    else:
        nib = np.empty((g, 128, n, 4), np.uint8)
        nib[..., 0::2] = words & 0xF
        nib[..., 1::2] = words >> 4
        vals = E2M1[nib]
    vals = vals * np.repeat(np.exp2(scales.astype(np.float64) - 127.0), 8, axis=1)[..., None]
    return vals.transpose(0, 1, 3, 2).reshape(g * 512, n)


K, T, J, R, C, N, E = 512, 2048, 256, 512, 512, 256, 1024


def setup_inputs():
    n = np.random.standard_normal
    idx = np.random.permutation(T)[:J]
    idx2 = np.random.permutation(T)[:J]
    idx3 = np.random.permutation(C)[:J]
    idx4 = np.random.permutation(C)[:J]
    idx5 = np.random.permutation(E)[:J]
    fk = mx_kscale(K)
    fr = mx_kscale(R)
    xtp = pack_weight(n((K, T)) / fk[:, None], "e5m2")
    wp = pack_weight(n((K, R)) * 1 / np.sqrt(K) * fk[:, None] * fr, "e2m1")
    wbp = pack_weight(n((R, N)) * 1 / np.sqrt(R) / fr[:, None], "e2m1")
    wsp = pack_weight(n((K, N)) * 1 / np.sqrt(K) * fk[:, None], "e2m1")
    return {
        "xt_words": xtp[0],
        "xt_scales": xtp[1],
        "w_words": wp[0],
        "w_scales": wp[1],
        "wb_words": wbp[0],
        "wb_scales": wbp[1],
        "ws_words": wsp[0],
        "ws_scales": wsp[1],
        "offs": striped(idx),
        "offs2": striped(idx2),
        "offs3": striped(idx3),
        "offs4": striped(idx4),
        "offs5": striped(idx5),
    }


def reference(xt_words, xt_scales, w_words, w_scales, wb_words, wb_scales, ws_words, ws_scales, offs, offs2, offs3, offs4, offs5):
    idx = unstriped(offs)
    idx2 = unstriped(offs2)
    idx3 = unstriped(offs3)
    idx4 = unstriped(offs4)
    idx5 = unstriped(offs5)
    xtu = unpack_weight(xt_words, xt_scales, "e5m2")
    wu = unpack_weight(w_words, w_scales, "e2m1")
    wbu = unpack_weight(wb_words, wb_scales, "e2m1")
    wsu = unpack_weight(ws_words, ws_scales, "e2m1")
    xtidxg = xtu[:, idx]
    a = wu.T @ xtidxg
    xtidx2g = xtu[:, idx2]
    b = wu.T @ xtidx2g
    pw = np.zeros((R, C))
    pw[:, idx3] = a
    hid = np.maximum(pw[:, idx4], b)
    hidq = mxq(hid, 0, "e4m3")
    p = wbu.T @ hidq + wsu.T @ xtidxg
    y = np.zeros((N, E))
    y[:, idx5] = p
    return y

from contextlib import ExitStack

import concourse.mybir as mybir

K, T, J, R, C, N, E = 512, 2048, 256, 512, 512, 256, 1024
FLOPS = 2 * K * R * J * 2 + 2 * R * N * J + 2 * K * N * J

F32 = mybir.dt.float32
BF16 = mybir.dt.bfloat16
I32 = mybir.dt.int32
U32 = mybir.dt.uint32
U16 = mybir.dt.uint16
U8 = mybir.dt.uint8
E4M3 = mybir.dt.float8_e4m3fn_x4
E5M2 = mybir.dt.float8_e5m2_x4
E2M1 = mybir.dt.float4_e2m1fn_x4
COPY = mybir.ActivationFunctionType.Copy
MAX = mybir.AluOpType.max

P = 128
PACK = 4
HALF = J // 2
LIST_COLS = J // 16


def tile_list_tied_board_skip_scattered_kernel(
    tc, xt_words, xt_scales, w_words, w_scales, wb_words, wb_scales, ws_words, ws_scales,
    offs, offs2, offs3, offs4, offs5, out,
):
    nc = tc.nc

    def move(engine, dst, src):
        if engine is nc.scalar:
            nc.scalar.activation(out=dst, in_=src, func=COPY)
        else:
            nc.vector.tensor_copy(out=dst, in_=src)

    def load_scale_rows(plane, rows):
        for q in range(4):
            nc.sync.dma_start(
                out=plane[32 * q : 32 * q + 4, :].bitcast(I32),
                in_=rows[0, 4 * q : 4 * q + 4, :].bitcast(I32),
            )

    with ExitStack() as ctx:
        sb = ctx.enter_context(tc.tile_pool(name="sb", bufs=1))
        ps = ctx.enter_context(tc.psum_pool(name="ps", bufs=1))

        lists = [sb.tile([P, LIST_COLS], U16, name="list%d" % i) for i in range(5)]
        first, second, put, pick, place = lists

        def half_of(lst, h):
            return lst[:, h * LIST_COLS // 2 : (h + 1) * LIST_COLS // 2]

        x_words = sb.tile([P, T], U32, align_bytes=64)
        x_plane = sb.tile([P, T], U8, align_bytes=64)
        w_raw = sb.tile([P, 2 * R], U8, align_bytes=64)
        weight_planes = sb.tile([P, R + 2 * N], U8, align_bytes=64)
        w_raw_plane = weight_planes[:, 0:R]
        ws_plane = weight_planes[:, R : R + N]
        wb_plane = weight_planes[:, R + N : R + 2 * N]
        ws_codes = sb.tile([P, 2 * N], U8, align_bytes=64)
        wb_codes = sb.tile([P, 2 * N], U8, align_bytes=64)

        nc.vector.memset(x_plane[:].bitcast(I32), 0)
        nc.vector.memset(weight_planes[:].bitcast(I32), 0)

        nc.scalar.dma_start(
            out=x_words[:].bitcast(I32),
            in_=xt_words[0].rearrange("p c r -> p (c r)").bitcast(I32),
        )
        nc.sync.dma_start(out=first[:], in_=offs)
        nc.sync.dma_start(out=w_raw[:].bitcast(I32), in_=w_words[0].bitcast(I32))
        load_scale_rows(x_plane, xt_scales)
        load_scale_rows(w_raw_plane, w_scales)
        nc.sync.dma_start(out=second[:], in_=offs2)
        nc.sync.dma_start(out=put[:], in_=offs3)
        nc.sync.dma_start(out=pick[:], in_=offs4)
        nc.sync.dma_start(out=ws_codes[:].bitcast(I32), in_=ws_words[0].bitcast(I32))
        load_scale_rows(ws_plane, ws_scales)
        nc.sync.dma_start(out=wb_codes[:].bitcast(I32), in_=wb_words[0].bitcast(I32))
        load_scale_rows(wb_plane, wb_scales)
        nc.sync.dma_start(out=place[:], in_=offs5)

        boards = [sb.tile([P, C], F32, name="board%d" % t) for t in range(PACK)]
        for board in boards:
            nc.vector.memset(board[:], 0.0)

        pages = [sb.tile([P, E], F32, name="page%d" % n) for n in range(N // P)]
        for page in pages:
            nc.vector.memset(page[:], 0.0)

        x1_plane = sb.tile([P, J], U8, align_bytes=64)
        x2_plane = sb.tile([P, J], U8, align_bytes=64)
        x1_words = sb.tile([P, J], U32, align_bytes=64)
        x2_words = sb.tile([P, J], U32, align_bytes=64)
        w_codes = sb.tile([P, 2 * R], U8, align_bytes=64)
        w_plane = sb.tile([P, R], U8, align_bytes=64)

        nc.vector.tensor_copy(
            out=w_codes[:].bitcast(U16).rearrange("p (t m) -> p t m", t=PACK),
            in_=w_raw[:].bitcast(U16).rearrange("p (m t) -> p t m", t=PACK),
        )
        nc.vector.tensor_copy(out=x1_plane[:], in_=x_plane[:].indirect(first[:]))
        nc.vector.tensor_copy(
            out=w_plane[:].rearrange("p (t m) -> p t m", t=PACK),
            in_=w_raw_plane.rearrange("p (m t) -> p t m", t=PACK),
        )
        nc.vector.tensor_copy(out=x1_words[:], in_=x_words[:].indirect(first[:]))
        nc.vector.tensor_copy(out=x2_plane[:], in_=x_plane[:].indirect(second[:]))
        nc.vector.tensor_copy(out=x2_words[:], in_=x_words[:].indirect(second[:]))

        def w_tile(t):
            return dict(
                lhsT=w_codes[:, 2 * P * t : 2 * P * (t + 1)].bitcast(E2M1),
                lhsT_scale=w_plane[:, P * t : P * (t + 1)],
            )

        owner = [nc.scalar, nc.vector, nc.scalar, nc.vector]

        a_banks = [ps.tile([P, J], F32, name="a_bank", tag="acc", bufs=4) for t in range(PACK)]
        for t in range(PACK):
            nc.tensor.matmul_mx(
                out=a_banks[t][:], rhs=x1_words[:].bitcast(E5M2), rhs_scale=x1_plane[:],
                start=True, stop=True, **w_tile(t),
            )
        b_banks = [ps.tile([P, PACK, HALF], F32, name="b_bank%d" % h) for h in range(2)]
        for h in range(2):
            cols = slice(h * HALF, (h + 1) * HALF)
            for t in range(PACK):
                nc.tensor.matmul_mx(
                    out=b_banks[h][:, t, :], rhs=x2_words[:, cols].bitcast(E5M2),
                    rhs_scale=x2_plane[:, cols], start=True, stop=True, **w_tile(t),
                )

        a_rows = [sb.tile([P, J], F32, name="a_rows%d" % t) for t in range(PACK)]
        for t in range(PACK):
            move(owner[t], a_rows[t][:], a_banks[t][:])
            move(owner[t], boards[t][:].indirect(put[:]), a_rows[t][:])

        picked = [sb.tile([P, PACK, HALF], F32, name="picked%d" % h) for h in range(2)]
        for t in range(PACK):
            move(owner[t], picked[0][:, t, :], boards[t][:].indirect(half_of(pick, 0)))
        for t in range(PACK):
            engine = nc.vector if t == PACK - 1 else nc.scalar
            move(engine, picked[1][:, t, :], boards[t][:].indirect(half_of(pick, 1)))

        p_banks = {}
        for h in range(2):
            cols = slice(h * HALF, (h + 1) * HALF)
            for n in range(N // P):
                p_banks[h, n] = ps.tile([P, HALF], F32, name="p_bank", tag="acc", bufs=4)
                nc.tensor.matmul_mx(
                    out=p_banks[h, n][:],
                    lhsT=ws_codes[:, 2 * P * n : 2 * P * (n + 1)].bitcast(E2M1),
                    lhsT_scale=ws_plane[:, P * n : P * (n + 1)],
                    rhs=x1_words[:, cols].bitcast(E5M2), rhs_scale=x1_plane[:, cols],
                    start=True, stop=False,
                )

        for h in range(2):
            hid = sb.tile([P, HALF * PACK], BF16, name="hid%d" % h, align_bytes=64)
            hid_codes = sb.tile([P, HALF], U32, name="hid_codes%d" % h, align_bytes=64)
            hid_plane = sb.tile([P, HALF], U8, name="hid_plane%d" % h, align_bytes=64)
            nc.vector.tensor_tensor(
                out=hid[:].rearrange("p (c i t) -> p c t i", i=4, t=PACK),
                in0=picked[h][:].rearrange("p t (c i) -> p c t i", i=4),
                in1=b_banks[h][:].rearrange("p t (c i) -> p c t i", i=4),
                op=MAX,
            )
            nc.vector.quantize_mx(out=hid_codes[:].bitcast(E4M3), scales=hid_plane[:], in_=hid[:])
            for n in range(N // P):
                nc.tensor.matmul_mx(
                    out=p_banks[h, n][:],
                    lhsT=wb_codes[:, 2 * P * n : 2 * P * (n + 1)].bitcast(E2M1),
                    lhsT_scale=wb_plane[:, P * n : P * (n + 1)],
                    rhs=hid_codes[:].bitcast(E4M3), rhs_scale=hid_plane[:],
                    start=False, stop=True,
                )

        for h in range(2):
            p_rows = [sb.tile([P, HALF], F32, name="p_rows%d%d" % (h, n)) for n in range(N // P)]
            for n in range(N // P):
                move(nc.scalar if h == 0 else owner[n], p_rows[n][:], p_banks[h, n][:])
            for n in range(N // P):
                move(owner[n], pages[n][:].indirect(half_of(place, h)), p_rows[n][:])

        for n in range(N // P):
            nc.sync.dma_start(out=out[P * n : P * (n + 1), :], in_=pages[n][:])
